import numpy as np
import ml_dtypes


def mxq(x, axis, fmt="e4m3"):
    dtype, down = {"e4m3": (ml_dtypes.float8_e4m3fn, 7), "e5m2": (ml_dtypes.float8_e5m2, 14)}[fmt]
    v = np.moveaxis(np.asarray(x, np.float32).astype(ml_dtypes.bfloat16).astype(np.float64), axis, -1)
    blocks = v.reshape(v.shape[:-1] + (-1, 32))
    amax = np.abs(blocks).max(-1, keepdims=True)
    byte = np.maximum(np.where(amax > 0, np.frexp(amax)[1] - 1 + 127, 0) - down, 1)
    scale = np.exp2(byte - 127.0)
    codes = (blocks / scale).astype(np.float32).astype(dtype).astype(np.float64)
    return np.moveaxis((codes * scale).reshape(v.shape), -1, axis)


WIDE = False


def mx_kscale(k):
    if not WIDE:
        return np.ones(k)
    levels = np.array([10, -10, 5, -5, 0])
    if k % 512:
        return np.exp2(np.random.permutation(np.resize(levels, k // 32))).repeat(32)
    a = np.empty((k // 512, 16))
    for p in range(k // 512):
        a[p, :8] = np.random.permutation(np.resize(levels, 8))
        for g in range(8):
            far = levels[np.abs(levels - a[p, g]) >= 10]
            a[p, g + 8] = far[np.random.randint(len(far))]
    return np.exp2(a.ravel()).repeat(32)


BF16 = ml_dtypes.bfloat16


def bf(x):
    return np.asarray(x, np.float32).astype(BF16)


def f64(x):
    return np.asarray(x).astype(np.float64)


L, P, B, D, T = 3, 2, 1024, 1024, 512


def scaled_message(n):
    w = np.exp(n - n.max(-1, keepdims=True))
    return n.shape[-1] * (w / w.sum(-1, keepdims=True))


def log_normalise(q):
    top = q.max(-1, keepdims=True)
    log_z = top + np.log(np.sum(np.exp(q - top), axis=-1, keepdims=True))
    return q - log_z + np.log(q.shape[-1])


def draw0():
    s = mx_kscale(D)
    t = np.stack([mx_kscale(T) for _ in range(P)])
    return {
        "x": bf(np.random.standard_normal((L, B, D)) * s),
        "we": bf(np.random.standard_normal((D, T)) / np.sqrt(D) / s[:, None]),
        "be": bf(0.3 * np.random.standard_normal(T)),
        "ends": bf(0.5 * np.random.standard_normal((P, T))),
        "gain": bf(np.random.standard_normal((P, T)) * t),
        "trans": bf(np.random.standard_normal((P, T, T)) * 3.5 / np.sqrt(T) / t[:, :, None]),
    }


def core(x, we, be, ends, gain, trans):
    e = (mxq(f64(x), 2, "e4m3") @ mxq(f64(we), 0, "e4m3")) + f64(be)
    en = f64(ends)
    n = np.stack([e[0] + en[0], e[2] + en[1]], axis=0)
    u = scaled_message(n)
    v = u * f64(gain)[:, None, :]
    m = mxq(v, 2, "e4m3") @ mxq(f64(trans), 1, "e4m3")
    c = np.log(np.maximum(1.0 + m / 16.0, 0.1))
    q = e[1] + c[0] + c[1]
    return log_normalise(q)


def e4m3fn_bytes(y):
    return np.clip(np.asarray(y, np.float64), -448.0, 448.0).astype(np.float32).astype(ml_dtypes.float8_e4m3fn).view(np.uint8)


def e4m3fn_values(b):
    return np.asarray(b, np.uint8).view(ml_dtypes.float8_e4m3fn).astype(np.float64)


def setup_inputs():
    d = draw0()
    x0 = np.asarray(d['x']).astype(np.float64)
    s = (np.max(np.abs(x0), axis=(0, 1), keepdims=True) / 448.0).astype(np.float32)
    out = {}
    for k, v in d.items():
        if k == 'x':
            out['x_bytes'] = e4m3fn_bytes(x0 / s.astype(np.float64))
            out['x_scale'] = s
        else:
            out[k] = v
    return out


def reference(x_bytes, x_scale, we, be, ends, gain, trans):
    return core(e4m3fn_values(x_bytes) * x_scale.astype(np.float64), we, be, ends, gain, trans)

@@ -1,0 +1,388 @@
+from contextlib import ExitStack
+
+import concourse.mybir as mybir
+from concourse.masks import make_identity
+
+L, B, D, T = 3, 1024, 1024, 512
+FLOPS = 2 * L * B * D * T + 2 * 2 * B * T * T
+
+F32 = mybir.dt.float32
+BF16 = mybir.dt.bfloat16
+U32 = mybir.dt.uint32
+U8 = mybir.dt.uint8
+FP8 = mybir.dt.float8_e4m3fn
+FP8X4 = mybir.dt.float8_e4m3fn_x4
+ACT = mybir.ActivationFunctionType
+ALU = mybir.AluOpType
+AXIS = mybir.AxisListType
+
+P = 128
+PACK = 4
+K_PASS = P * PACK
+PASSES = D // K_PASS
+GROUP = 512
+TILES = GROUP // P
+CHUNKS = T // P
+HALVES = B // GROUP
+MIDDLE = 1
+GROUPS = [(0, 0), (2, 0), (1, 0), (0, 1), (2, 1), (1, 1)]
+N_TILES = len(GROUPS) * TILES
+
+LAG_QUANT = 5
+LAG_ROWS = 9
+MSG_START = 25
+TRANS_START = 10
+GAIN_TICK = 8
+LAG_V = 2
+MSG_TAG = "xt"
+BANKS = {"xt": 2, "et": 2, "rows": 3, "vt": 1}
+LAG_G = 1
+MSG_STEP = 1
+SPLIT_TAIL = 2
+FLOOR_SET = (0, 1, 2, 3)
+DOUBLE = (6, 7)
+SKIP = (9, 13, 17, 21)
+X_BUFS = 8
+LN_PER = 2
+LEAD = 2
+SCALAR_FLOORS = 4
+
+
+def tile_chunkflooredmessagemiddlescore_kernel(tc, x_bytes, x_scale, we, be, ends, gain, trans, out):
+    nc = tc.nc
+    with ExitStack() as ctx:
+        keep = ctx.enter_context(tc.tile_pool(name="keep", bufs=1))
+        work = ctx.enter_context(tc.tile_pool(name="work", bufs=2))
+        psum = ctx.enter_context(tc.psum_pool(name="psum", bufs=1))
+        ctx.enter_context(tc.manual_schedule())
+
+        def bank(tag, shape=(P, T), dtype=F32):
+            return psum.tile(list(shape), dtype, name=tag, tag=tag, bufs=BANKS[tag])
+
+        xb = [keep.tile([P, TILES, D], U8, name="x_bytes_%d" % g, align_bytes=64) for g in range(len(GROUPS))]
+        w_raw = [keep.tile([P, PACK, T], BF16, name="w_raw_%d" % i, align_bytes=64) for i in range(4)]
+        scale_cols = keep.tile([P, 8], F32, name="scale_cols")
+        bias_rows = keep.tile([P, P], BF16, name="bias_rows")
+        gain_cols = keep.tile([P, 2, PACK], BF16, name="gain_cols")
+        ident32 = keep.tile([P, P], F32, name="ident32")
+        ident16 = keep.tile([P, P], BF16, name="ident16")
+
+        def x_rows(g):
+            l, h = GROUPS[g]
+            return x_bytes[l, h * GROUP:(h + 1) * GROUP, :].rearrange("(p j) k -> p j k", j=TILES)
+
+        def load_w(i):
+            rows = we[i * K_PASS:(i + 1) * K_PASS, :] if i < PASSES else trans[i - PASSES]
+            nc.sync.dma_start(out=w_raw[i][:], in_=rows.rearrange("(p j) n -> p j n", j=PACK))
+
+        make_identity(nc, ident32[:])
+        make_identity(nc, ident16[:])
+        nc.vector.memset(bias_rows[:], 0.0)
+        nc.sync.dma_start(out=scale_cols[:], in_=x_scale.rearrange("a b (p c) -> p (a b c)", c=8))
+        nc.sync.dma_start(out=xb[0][:, 0, :], in_=x_rows(0)[:, 0, :])
+        load_w(0)
+        nc.sync.dma_start(out=xb[0][:, 1, :], in_=x_rows(0)[:, 1, :])
+        load_w(1)
+        nc.sync.dma_start(out=xb[0][:, 2:4, :], in_=x_rows(0)[:, 2:4, :])
+        nc.sync.dma_start(out=xb[1][:], in_=x_rows(1))
+        nc.sync.dma_start(out=bias_rows[0:CHUNKS, :], in_=be.rearrange("(c q) -> c q", q=P))
+        nc.sync.dma_start(out=bias_rows[CHUNKS:3 * CHUNKS, :], in_=ends.rearrange("e (c q) -> (e c) q", q=P))
+        nc.sync.dma_start(out=gain_cols[:], in_=gain.rearrange("g (m c) -> m g c", c=PACK))
+        nc.sync.dma_start(out=xb[2][:], in_=x_rows(2))
+        load_w(2)
+        load_w(3)
+        for g in range(3, len(GROUPS)):
+            nc.sync.dma_start(out=xb[g][:], in_=x_rows(g))
+
+        scale_all = keep.tile([P, D], F32, name="scale_all")
+        scale_view = scale_all[:].rearrange("p (q h c) -> p h q c", h=2, c=4)
+        for h in range(2):
+            spread = bank("rows")
+            for c in range(4):
+                col = 4 * h + c
+                nc.tensor.transpose(spread[:, c * P:(c + 1) * P], scale_cols[:, col:col + 1].to_broadcast([P, P]), ident32[:])
+            src = spread[:].rearrange("p (c q) -> p q c", c=4)
+            if h == 0:
+                nc.vector.tensor_copy(out=scale_view[:, h], in_=src)
+            else:
+                nc.scalar.copy(out=scale_view[:, h], in_=src)
+
+        w_codes = [keep.tile([P, T], U32, name="w_codes_%d" % i, align_bytes=64) for i in range(4)]
+        w_scales = [keep.tile([P, T], U8, name="w_scales_%d" % i, align_bytes=64) for i in range(4)]
+        w_grouped = {}
+
+        def interleave_w(i, part, parts):
+            if part == 0:
+                w_grouped[i] = work.tile([P, T, PACK], BF16, name="w_grouped", align_bytes=64)
+            cols = slice(part * T // parts, (part + 1) * T // parts)
+            nc.scalar.copy(
+                out=w_grouped[i][:, cols, :].rearrange("p (c i) t -> p c t i", i=4),
+                in_=w_raw[i][:, :, cols].rearrange("p t (c i) -> p c t i", i=4),
+            )
+
+        def quantize_w(i):
+            nc.vector.quantize_mx(out=w_codes[i][:].bitcast(FP8X4), scales=w_scales[i][:],
+                                  in_=w_grouped[i][:].rearrange("p n t -> p (n t)"))
+
+        bias_raw = keep.tile([P, 3 * CHUNKS], F32, name="bias_raw")
+        bias_end = keep.tile([P, 2 * CHUNKS], F32, name="bias_end")
+
+        def make_bias():
+            turned = bank("vt", (P, P), BF16)
+            nc.tensor.transpose(turned[:], bias_rows[:], ident16[:])
+            nc.scalar.copy(out=bias_raw[:], in_=turned[:, 0:3 * CHUNKS])
+            for e in range(2):
+                nc.gpsimd.tensor_tensor(out=bias_end[:, e * CHUNKS:(e + 1) * CHUNKS], in0=bias_raw[:, 0:CHUNKS],
+                                        in1=bias_raw[:, (e + 1) * CHUNKS:(e + 2) * CHUNKS], op=ALU.add)
+
+        gain_all = keep.tile([P, 2, T], F32, name="gain_all")
+
+        def make_gain():
+            spread = bank("vt", (P, 2, PACK, P), BF16)
+            for e in range(2):
+                for c in range(PACK):
+                    nc.tensor.transpose(spread[:, e, c, :], gain_cols[:, e, c:c + 1].to_broadcast([P, P]), ident16[:])
+            for e in range(2):
+                nc.scalar.activation(out=gain_all[:, e, :].rearrange("p (u m s) -> p u m s", u=2, s=2),
+                                     in_=spread[:, e].rearrange("p (u s) m -> p u m s", u=2),
+                                     func=ACT.Copy, scale=float(T))
+
+        neg_max = keep.tile([P, N_TILES], F32, name="neg_max")
+        sums = keep.tile([P, N_TILES], F32, name="sums")
+        inv_sums = keep.tile([P, N_TILES], F32, name="inv_sums")
+        total = keep.tile([P, HALVES * TILES], F32, name="total")
+        inv_total = keep.tile([P, HALVES * TILES], F32, name="inv_total")
+        x16, x_grouped, x_codes, x_scales, x_turned = {}, {}, {}, {}, {}
+        e_bank, scores_t, rows, weights, neg_scores, v16 = {}, {}, {}, {}, {}, {}
+        v_turned, v_grouped, v_codes, v_scales = {}, {}, {}, {}
+        m_bank, floor0, floor1, product = {}, {}, {}, {}
+
+        def scale_x(n):
+            g, j = divmod(n, TILES)
+            x16[n] = work.tile([P, D], BF16, name="x16", bufs=X_BUFS, align_bytes=64)
+            nc.vector.tensor_tensor(out=x16[n][:], in0=xb[g][:, j, :].bitcast(FP8), in1=scale_all[:], op=ALU.mult)
+
+        def turn_x(n):
+            words = x16[n][:].bitcast(F32)
+            x_turned[n] = bank("xt")
+            for k in range(PASSES):
+                for u in range(2):
+                    i = 2 * k + u
+                    nc.tensor.transpose(x_turned[n][:, i * P:(i + 1) * P], words[:, 256 * k + u:256 * (k + 1):2], ident32[:])
+
+        def copy_x(n):
+            g, j = divmod(n, TILES)
+            if j == 0:
+                x_grouped[g] = work.tile([P, PASSES, GROUP * PACK], BF16, name="x_grouped", align_bytes=64)
+            dst = x_grouped[g][:].bitcast(F32).rearrange("p k (r u) -> p k r u", u=2)[:, :, j * P:(j + 1) * P, :]
+            nc.scalar.copy(out=dst, in_=x_turned[n][:].rearrange("p (k u r) -> p k r u", k=PASSES, u=2))
+
+        def quantize_x(g):
+            x_codes[g] = work.tile([P, PASSES, GROUP], U32, name="x_codes", align_bytes=64)
+            x_scales[g] = work.tile([P, PASSES, GROUP], U8, name="x_scales", align_bytes=64)
+            for k in range(PASSES):
+                nc.vector.quantize_mx(out=x_codes[g][:, k, :].bitcast(FP8X4), scales=x_scales[g][:, k, :],
+                                      in_=x_grouped[g][:, k, :])
+
+        def emit(g, c):
+            e_bank[g, c] = bank("et")
+            cols = slice(c * P, (c + 1) * P)
+            for k in range(PASSES):
+                nc.tensor.matmul_mx(out=e_bank[g, c][:], lhsT=w_codes[k][:, cols].bitcast(FP8X4), lhsT_scale=w_scales[k][:, cols],
+                                    rhs=x_codes[g][:, k, :].bitcast(FP8X4), rhs_scale=x_scales[g][:, k, :],
+                                    start=(k == 0), stop=(k == PASSES - 1))
+
+        def add_bias(g, c):
+            l = GROUPS[g][0]
+            if c == 0:
+                scores_t[g] = work.tile([P, CHUNKS, GROUP], F32, name="scores_t")
+            col = bias_raw[:, c:c + 1] if l == MIDDLE else bias_end[:, (l // 2) * CHUNKS + c:(l // 2) * CHUNKS + c + 1]
+            nc.scalar.activation(out=scores_t[g][:, c, :], in_=e_bank[g, c][:], func=ACT.Identity, bias=col)
+
+        def turn_scores(n):
+            g, j = divmod(n, TILES)
+            rows[n] = bank("rows")
+            for c in range(CHUNKS):
+                nc.tensor.transpose(rows[n][:, c * P:(c + 1) * P], scores_t[g][:, c, j * P:(j + 1) * P], ident32[:])
+
+        def row_max(n):
+            if GROUPS[n // TILES][0] == MIDDLE:
+                neg_scores[n] = keep.tile([P, T], F32, name="neg_scores_%d" % n)
+                nc.vector.tensor_scalar(out=neg_scores[n][:], in0=rows[n][:], scalar1=-1.0, scalar2=None,
+                                        op0=ALU.mult, op1=ALU.min, accum_out=neg_max[:, n:n + 1])
+            else:
+                nc.vector.tensor_reduce(out=neg_max[:, n:n + 1], in_=rows[n][:], axis=AXIS.X, op=ALU.max, negate=True)
+
+        def exponentiate(n):
+            if GROUPS[n // TILES][0] == MIDDLE:
+                weights[n] = keep.tile([P, T], F32, name="weights_%d" % n)
+                nc.scalar.activation(out=weights[n][:], in_=rows[n][:], func=ACT.Exp, bias=neg_max[:, n:n + 1])
+            else:
+                weights[n] = work.tile([P, T], F32, name="weights", bufs=4)
+                nc.scalar.activation(out=weights[n][:].rearrange("p (u m s) -> p u m s", u=2, s=2),
+                                     in_=rows[n][:].rearrange("p (m u s) -> p u m s", u=2, s=2),
+                                     func=ACT.Exp, bias=neg_max[:, n:n + 1], accum_out=sums[:, n:n + 1])
+
+        def invert_sum(n):
+            nc.vector.reciprocal(out=inv_sums[:, n:n + 1], in_=sums[:, n:n + 1])
+
+        def make_v(n):
+            e = GROUPS[n // TILES][0] // 2
+            v16[n] = work.tile([P, T], BF16, name="v16", bufs=4, align_bytes=64)
+            nc.vector.scalar_tensor_tensor(out=v16[n][:], in0=weights[n][:], scalar=inv_sums[:, n:n + 1],
+                                           in1=gain_all[:, e, :], op0=ALU.mult, op1=ALU.mult)
+
+        def turn_v(pair):
+            v_turned[pair] = bank("vt")
+            for i in range(2):
+                words = v16[2 * pair + i][:].bitcast(F32)
+                for u in range(2):
+                    s = 2 * i + u
+                    nc.tensor.transpose(v_turned[pair][:, s * P:(s + 1) * P], words[:, u * P:(u + 1) * P], ident32[:])
+
+        def copy_v(pair):
+            v_grouped[pair] = work.tile([P, 2 * P * PACK], BF16, name="v_grouped", align_bytes=64)
+            nc.scalar.copy(out=v_grouped[pair][:].bitcast(F32).rearrange("p (i r u) -> p i r u", i=2, u=2),
+                           in_=v_turned[pair][:].rearrange("p (i u r) -> p i r u", i=2, u=2))
+
+        def quantize_v(pair):
+            v_codes[pair] = keep.tile([P, 2 * P], U32, name="v_codes_%d" % pair, align_bytes=64)
+            v_scales[pair] = keep.tile([P, 2 * P], U8, name="v_scales_%d" % pair, align_bytes=64)
+            nc.vector.quantize_mx(out=v_codes[pair][:].bitcast(FP8X4), scales=v_scales[pair][:], in_=v_grouped[pair][:])
+
+        def tile_of(l, o):
+            h, j = divmod(o, TILES)
+            return GROUPS.index((l, h)) * TILES + j
+
+        def pass_messages(o):
+            for e in range(2):
+                pair, i = divmod(tile_of(2 * e, o), 2)
+                cols = slice(i * P, (i + 1) * P)
+                m_bank[o, e] = bank(MSG_TAG)
+                nc.tensor.matmul_mx(out=m_bank[o, e][:], lhsT=v_codes[pair][:, cols].bitcast(FP8X4), lhsT_scale=v_scales[pair][:, cols],
+                                    rhs=w_codes[PASSES + e][:].bitcast(FP8X4), rhs_scale=w_scales[PASSES + e][:],
+                                    start=True, stop=True)
+
+        def floor_messages(o):
+            floor0[o] = work.tile([P, T], F32, name="floor0", bufs=3)
+            floor1[o] = work.tile([P, T], F32, name="floor1", bufs=3)
+            if o in FLOOR_SET:
+                nc.scalar.activation(out=floor1[o][:], in_=m_bank[o, 1][:], func=ACT.Relu, bias=14.4)
+            nc.scalar.activation(out=floor0[o][:], in_=m_bank[o, 0][:], func=ACT.Relu, scale=1.0 / 16.0, bias=0.9)
+            if o in FLOOR_SET:
+                nc.scalar.activation(out=floor1[o][:], in_=floor1[o][:], func=ACT.Identity, bias=1.6)
+            else:
+                nc.vector.tensor_scalar(out=floor1[o][:], in0=m_bank[o, 1][:], scalar1=-14.4, scalar2=16.0, op0=ALU.max, op1=ALU.add)
+
+        def multiply_floors(o):
+            product[o] = keep.tile([P, T], F32, name="product_%d" % o)
+            nc.vector.scalar_tensor_tensor(out=product[o][:], in0=floor0[o][:], scalar=0.1, in1=floor1[o][:],
+                                           op0=ALU.add, op1=ALU.mult)
+
+        def sum_tags(o):
+            w = weights[tile_of(MIDDLE, o)]
+            nc.vector.scalar_tensor_tensor(out=w[:], in0=w[:], scalar=1.0 / T, in1=product[o][:],
+                                           op0=ALU.mult, op1=ALU.mult, accum_out=total[:, o:o + 1])
+
+        out_rows = out.rearrange("(h p j) t -> h j p t", p=P, j=TILES)
+
+        def invert_total(o0, o1):
+            nc.vector.reciprocal(out=inv_total[:, o0:o1], in_=total[:, o0:o1])
+
+        def take_log(o):
+            nc.scalar.activation(out=product[o][:], in_=product[o][:], func=ACT.Ln, scale=inv_total[:, o:o + 1])
+
+        def finish(o):
+            n = tile_of(MIDDLE, o)
+            nc.vector.scalar_tensor_tensor(out=product[o][:], in0=product[o][:], scalar=neg_max[:, n:n + 1],
+                                           in1=neg_scores[n][:], op0=ALU.add, op1=ALU.subtract)
+            nc.sync.dma_start(out=out_rows[o // TILES, o % TILES], in_=product[o][:])
+
+        def log_tick(o):
+            return max(N_TILES + LAG_ROWS + o // LN_PER, sum_tick(o) + 1)
+
+        def message_tick(o):
+            ready = max(tile_of(0, o | 1), tile_of(2, o | 1)) + LAG_ROWS + LAG_V + 3
+            return max(MSG_START + MSG_STEP * o, ready + (o & 1))
+
+        def sum_tick(o):
+            return max(message_tick(o) + LAG_G + 1, tile_of(MIDDLE, o) + LAG_ROWS + 1)
+
+        def is_end(n):
+            return 0 <= n < N_TILES and GROUPS[n // TILES][0] != MIDDLE
+
+        interleave_w(0, 0, 1)
+        interleave_w(1, 0, 1)
+        for n in range(LEAD):
+            scale_x(n)
+        outs = range(HALVES * TILES)
+        last_tick = max(log_tick(o) for o in outs) + 1
+        for t in range(last_tick + 1):
+            a = t - LAG_ROWS
+            b = a - LAG_V
+            g, c = divmod(t - LAG_QUANT, TILES)
+            emitting = 0 <= g < len(GROUPS)
+            pair_turn = (b - 1) // 2 if (b - 1) % 2 == 1 and is_end(b - 1) else None
+            pair_quant = (b - 2) // 2 if (b - 2) % 2 == 1 and is_end(b - 2) else None
+            messages = [o for o in outs if message_tick(o) == t]
+            if 0 <= a - 1 < N_TILES:
+                exponentiate(a - 1)
+            for o in outs:
+                if log_tick(o) - 1 == t - 1:
+                    take_log(o)
+            if 0 <= a < N_TILES:
+                turn_scores(a)
+            if emitting and c == 0:
+                quantize_x(g)
+            if 0 <= t - 1 < N_TILES:
+                turn_x(t - 1)
+            for rep in range(2 if t in DOUBLE else 0 if t in SKIP else 1):
+                if len(x16) < N_TILES:
+                    scale_x(len(x16))
+            if t in (2, 4):
+                quantize_w(t // 2 - 1)
+            if t == 3:
+                make_bias()
+            if t == GAIN_TICK:
+                make_gain()
+            if pair_turn is not None:
+                turn_v(pair_turn)
+            if 0 <= t - 1 < N_TILES:
+                copy_x(t - 1)
+            if is_end(b):
+                invert_sum(b)
+            if 0 <= a < N_TILES:
+                row_max(a)
+            if is_end(b):
+                make_v(b)
+            if pair_quant is not None:
+                quantize_v(pair_quant)
+            if pair_turn is not None:
+                copy_v(pair_turn)
+            if emitting:
+                emit(g, c)
+            for o in messages:
+                pass_messages(o)
+            if emitting:
+                add_bias(g, c)
+            if 0 <= t - TRANS_START < 8:
+                interleave_w(PASSES + (t - TRANS_START) // 4, (t - TRANS_START) % 4, 4)
+            if t - TRANS_START in (5, 9):
+                quantize_w(PASSES + (t - TRANS_START - 5) // 4)
+            for o in messages:
+                floor_messages(o)
+            for o in outs:
+                if sum_tick(o) == t:
+                    sum_tags(o)
+            for o in outs:
+                if message_tick(o) + LAG_G == t:
+                    multiply_floors(o)
+
+            for o in outs:
+                if sum_tick(o) == t and o >= TILES:
+                    invert_total(o, o + 1)
+            if sum_tick(TILES - 1) + 1 == t:
+                invert_total(0, TILES)
+            for o in outs:
+                if log_tick(o) == t:
+                    finish(o)

@@ -23,29 +23,32 @@ PASSES = D // K_PASS
 GROUP = 512
 TILES = GROUP // P
 CHUNKS = T // P
-HALVES = B // GROUP
 MIDDLE = 1
-GROUPS = [(0, 0), (2, 0), (1, 0), (0, 1), (2, 1), (1, 1)]
+GROUPS = [(0, 0), (2, 0), (0, 1), (2, 1), (MIDDLE, 0), (MIDDLE, 1)]
 N_TILES = len(GROUPS) * TILES
+N_OUT = B // P
 
-LAG_QUANT = 5
-LAG_ROWS = 9
-MSG_START = 25
-TRANS_START = 10
-GAIN_TICK = 8
-LAG_V = 2
-MSG_TAG = "xt"
-BANKS = {"xt": 2, "et": 2, "rows": 3, "vt": 1}
-LAG_G = 1
-MSG_STEP = 1
-SPLIT_TAIL = 2
-FLOOR_SET = (0, 1, 2, 3)
-DOUBLE = (6, 7)
-SKIP = (9, 13, 17, 21)
-X_BUFS = 8
-LN_PER = 2
-LEAD = 2
-SCALAR_FLOORS = 4
+EMIT_AT = TILES + 1
+BIAS_AT = EMIT_AT + 1
+TURN_SCORES_AT = BIAS_AT + CHUNKS
+MAX_AT = TURN_SCORES_AT + 1
+EXP_AT = MAX_AT + 1
+MAKE_V_AT = EXP_AT + 1
+TURN_V_AT = MAKE_V_AT + 1
+COPY_V_AT = TURN_V_AT + 1
+QUANT_V_AT = COPY_V_AT + 1
+PASS_AT = QUANT_V_AT + 1
+DOUBLE_TICKS = range(BIAS_AT, TURN_SCORES_AT)
+X_LEAD = 2
+WE_QUANT_TICKS = (2, 4)
+BIAS_SETUP_TICK = BIAS_AT - 3
+GAIN_SETUP_TICK = MAKE_V_AT - 2
+TRANS_TICK = 4
+TRANS_PARTS = 4
+SCALAR_FLOORS_FROM = 2
+LOGS_PER_TICK = 2
+
+BANKS = {"x": 2, "emit": 2, "rows": 3, "v": 1}
 
 
 def tile_chunkflooredmessagemiddlescore_kernel(tc, x_bytes, x_scale, we, be, ends, gain, trans, out):
@@ -59,162 +62,185 @@ def tile_chunkflooredmessagemiddlescore_kernel(tc, x_bytes, x_scale, we, be, end
         def bank(tag, shape=(P, T), dtype=F32):
             return psum.tile(list(shape), dtype, name=tag, tag=tag, bufs=BANKS[tag])
 
-        xb = [keep.tile([P, TILES, D], U8, name="x_bytes_%d" % g, align_bytes=64) for g in range(len(GROUPS))]
-        w_raw = [keep.tile([P, PACK, T], BF16, name="w_raw_%d" % i, align_bytes=64) for i in range(4)]
-        scale_cols = keep.tile([P, 8], F32, name="scale_cols")
+        n_weights = PASSES + 2
+        x_raw = [keep.tile([P, TILES, D], U8, name="x_bytes_%d" % g, align_bytes=64) for g in range(len(GROUPS))]
+        w_raw = [keep.tile([P, PACK, T], BF16, name="w_raw_%d" % i, align_bytes=64) for i in range(n_weights)]
+        scale_cols = keep.tile([P, PASSES * PACK], F32, name="scale_cols")
         bias_rows = keep.tile([P, P], BF16, name="bias_rows")
         gain_cols = keep.tile([P, 2, PACK], BF16, name="gain_cols")
         ident32 = keep.tile([P, P], F32, name="ident32")
         ident16 = keep.tile([P, P], BF16, name="ident16")
 
-        def x_rows(g):
-            l, h = GROUPS[g]
-            return x_bytes[l, h * GROUP:(h + 1) * GROUP, :].rearrange("(p j) k -> p j k", j=TILES)
+        def load_x(g, j0, j1):
+            position, half = GROUPS[g]
+            tokens = x_bytes[position, half * GROUP:(half + 1) * GROUP, :].rearrange("(p j) k -> p j k", j=TILES)
+            nc.sync.dma_start(out=x_raw[g][:, j0:j1, :], in_=tokens[:, j0:j1, :])
 
         def load_w(i):
-            rows = we[i * K_PASS:(i + 1) * K_PASS, :] if i < PASSES else trans[i - PASSES]
-            nc.sync.dma_start(out=w_raw[i][:], in_=rows.rearrange("(p j) n -> p j n", j=PACK))
+            matrix = we[i * K_PASS:(i + 1) * K_PASS, :] if i < PASSES else trans[i - PASSES]
+            nc.sync.dma_start(out=w_raw[i][:], in_=matrix.rearrange("(p t) n -> p t n", t=PACK))
 
         make_identity(nc, ident32[:])
         make_identity(nc, ident16[:])
         nc.vector.memset(bias_rows[:], 0.0)
-        nc.sync.dma_start(out=scale_cols[:], in_=x_scale.rearrange("a b (p c) -> p (a b c)", c=8))
-        nc.sync.dma_start(out=xb[0][:, 0, :], in_=x_rows(0)[:, 0, :])
+        nc.sync.dma_start(out=scale_cols[:].rearrange("p (ps t) -> p ps t", ps=PASSES),
+                          in_=x_scale.rearrange("a b (ps p t) -> p (a b ps) t", ps=PASSES, t=PACK))
+        load_x(0, 0, 1)
         load_w(0)
-        nc.sync.dma_start(out=xb[0][:, 1, :], in_=x_rows(0)[:, 1, :])
+        load_x(0, 1, 2)
         load_w(1)
-        nc.sync.dma_start(out=xb[0][:, 2:4, :], in_=x_rows(0)[:, 2:4, :])
-        nc.sync.dma_start(out=xb[1][:], in_=x_rows(1))
+        load_x(0, 2, TILES)
+        load_x(1, 0, TILES)
         nc.sync.dma_start(out=bias_rows[0:CHUNKS, :], in_=be.rearrange("(c q) -> c q", q=P))
         nc.sync.dma_start(out=bias_rows[CHUNKS:3 * CHUNKS, :], in_=ends.rearrange("e (c q) -> (e c) q", q=P))
-        nc.sync.dma_start(out=gain_cols[:], in_=gain.rearrange("g (m c) -> m g c", c=PACK))
-        nc.sync.dma_start(out=xb[2][:], in_=x_rows(2))
-        load_w(2)
-        load_w(3)
+        nc.sync.dma_start(out=gain_cols[:], in_=gain.rearrange("e (p t) -> p e t", t=PACK))
+        load_w(PASSES)
+        load_x(2, 0, TILES)
+        load_w(PASSES + 1)
         for g in range(3, len(GROUPS)):
-            nc.sync.dma_start(out=xb[g][:], in_=x_rows(g))
+            load_x(g, 0, TILES)
 
         scale_all = keep.tile([P, D], F32, name="scale_all")
-        scale_view = scale_all[:].rearrange("p (q h c) -> p h q c", h=2, c=4)
-        for h in range(2):
+        for ps in range(PASSES):
             spread = bank("rows")
-            for c in range(4):
-                col = 4 * h + c
-                nc.tensor.transpose(spread[:, c * P:(c + 1) * P], scale_cols[:, col:col + 1].to_broadcast([P, P]), ident32[:])
-            src = spread[:].rearrange("p (c q) -> p q c", c=4)
-            if h == 0:
-                nc.vector.tensor_copy(out=scale_view[:, h], in_=src)
+            for t in range(PACK):
+                col = PACK * ps + t
+                nc.tensor.transpose(spread[:, t * P:(t + 1) * P], scale_cols[:, col:col + 1].to_broadcast([P, P]), ident32[:])
+            dst = scale_all[:, ps * K_PASS:(ps + 1) * K_PASS].rearrange("p (q t) -> p q t", t=PACK)
+            src = spread[:].rearrange("p (t q) -> p q t", t=PACK)
+            if ps == 0:
+                nc.vector.tensor_copy(out=dst, in_=src)
             else:
-                nc.scalar.copy(out=scale_view[:, h], in_=src)
+                nc.scalar.copy(out=dst, in_=src)
 
-        w_codes = [keep.tile([P, T], U32, name="w_codes_%d" % i, align_bytes=64) for i in range(4)]
-        w_scales = [keep.tile([P, T], U8, name="w_scales_%d" % i, align_bytes=64) for i in range(4)]
+        w_codes = [keep.tile([P, T], U32, name="w_codes_%d" % i, align_bytes=64) for i in range(n_weights)]
+        w_scales = [keep.tile([P, T], U8, name="w_scales_%d" % i, align_bytes=64) for i in range(n_weights)]
         w_grouped = {}
 
         def interleave_w(i, part, parts):
             if part == 0:
                 w_grouped[i] = work.tile([P, T, PACK], BF16, name="w_grouped", align_bytes=64)
             cols = slice(part * T // parts, (part + 1) * T // parts)
-            nc.scalar.copy(
-                out=w_grouped[i][:, cols, :].rearrange("p (c i) t -> p c t i", i=4),
-                in_=w_raw[i][:, :, cols].rearrange("p t (c i) -> p c t i", i=4),
-            )
+            nc.scalar.copy(out=w_grouped[i][:, cols, :].rearrange("p (c r) t -> p c t r", r=4),
+                           in_=w_raw[i][:, :, cols].rearrange("p t (c r) -> p c t r", r=4))
 
         def quantize_w(i):
             nc.vector.quantize_mx(out=w_codes[i][:].bitcast(FP8X4), scales=w_scales[i][:],
                                   in_=w_grouped[i][:].rearrange("p n t -> p (n t)"))
 
-        bias_raw = keep.tile([P, 3 * CHUNKS], F32, name="bias_raw")
-        bias_end = keep.tile([P, 2 * CHUNKS], F32, name="bias_end")
+        bias_cols = keep.tile([P, 3 * CHUNKS], F32, name="bias_cols")
+        end_bias = keep.tile([P, 2 * CHUNKS], F32, name="end_bias")
 
-        def make_bias():
-            turned = bank("vt", (P, P), BF16)
-            nc.tensor.transpose(turned[:], bias_rows[:], ident16[:])
-            nc.scalar.copy(out=bias_raw[:], in_=turned[:, 0:3 * CHUNKS])
+        bias_bank = []
+
+        def turn_bias():
+            bias_bank.append(bank("v", (P, P), BF16))
+            nc.tensor.transpose(bias_bank[0][:], bias_rows[:], ident16[:])
+
+        def copy_bias():
+            nc.scalar.copy(out=bias_cols[:], in_=bias_bank[0][:, 0:3 * CHUNKS])
             for e in range(2):
-                nc.gpsimd.tensor_tensor(out=bias_end[:, e * CHUNKS:(e + 1) * CHUNKS], in0=bias_raw[:, 0:CHUNKS],
-                                        in1=bias_raw[:, (e + 1) * CHUNKS:(e + 2) * CHUNKS], op=ALU.add)
+                nc.gpsimd.tensor_tensor(out=end_bias[:, e * CHUNKS:(e + 1) * CHUNKS], in0=bias_cols[:, 0:CHUNKS],
+                                        in1=bias_cols[:, (e + 1) * CHUNKS:(e + 2) * CHUNKS], op=ALU.add)
 
         gain_all = keep.tile([P, 2, T], F32, name="gain_all")
+        gain_bank = []
 
-        def make_gain():
-            spread = bank("vt", (P, 2, PACK, P), BF16)
+        def spread_gain():
+            gain_bank.append(bank("v", (P, 2, PACK, P), BF16))
             for e in range(2):
-                for c in range(PACK):
-                    nc.tensor.transpose(spread[:, e, c, :], gain_cols[:, e, c:c + 1].to_broadcast([P, P]), ident16[:])
+                for t in range(PACK):
+                    nc.tensor.transpose(gain_bank[0][:, e, t, :], gain_cols[:, e, t:t + 1].to_broadcast([P, P]), ident16[:])
+
+        def copy_gain():
             for e in range(2):
                 nc.scalar.activation(out=gain_all[:, e, :].rearrange("p (u m s) -> p u m s", u=2, s=2),
-                                     in_=spread[:, e].rearrange("p (u s) m -> p u m s", u=2),
+                                     in_=gain_bank[0][:, e].rearrange("p (u s) m -> p u m s", u=2),
                                      func=ACT.Copy, scale=float(T))
 
         neg_max = keep.tile([P, N_TILES], F32, name="neg_max")
         sums = keep.tile([P, N_TILES], F32, name="sums")
         inv_sums = keep.tile([P, N_TILES], F32, name="inv_sums")
-        total = keep.tile([P, HALVES * TILES], F32, name="total")
-        inv_total = keep.tile([P, HALVES * TILES], F32, name="inv_total")
-        x16, x_grouped, x_codes, x_scales, x_turned = {}, {}, {}, {}, {}
-        e_bank, scores_t, rows, weights, neg_scores, v16 = {}, {}, {}, {}, {}, {}
-        v_turned, v_grouped, v_codes, v_scales = {}, {}, {}, {}
-        m_bank, floor0, floor1, product = {}, {}, {}, {}
+        total = keep.tile([P, N_OUT], F32, name="total")
+        inv_total = keep.tile([P, N_OUT], F32, name="inv_total")
+        x16, x_turned, x_grouped, x_codes, x_scales = {}, {}, {}, {}, {}
+        emission, scores_t, rows, weights = {}, {}, {}, {}
+        v16, v_turned, v_grouped, v_codes, v_scales = {}, {}, {}, {}, {}
+        message, floor0, floor1, product, middle_rows = {}, {}, {}, {}, {}
+        out_rows = out.rearrange("(h p j) t -> h j p t", p=P, j=TILES)
+
+        def is_tile(n):
+            return 0 <= n < N_TILES
+
+        def is_middle(n):
+            return GROUPS[n // TILES][0] == MIDDLE
+
+        def closes_pair(n):
+            return is_tile(n) and not is_middle(n) and n % 2 == 1
+
+        def tile_of(position, o):
+            half, j = divmod(o, TILES)
+            return GROUPS.index((position, half)) * TILES + j
 
         def scale_x(n):
             g, j = divmod(n, TILES)
-            x16[n] = work.tile([P, D], BF16, name="x16", bufs=X_BUFS, align_bytes=64)
-            nc.vector.tensor_tensor(out=x16[n][:], in0=xb[g][:, j, :].bitcast(FP8), in1=scale_all[:], op=ALU.mult)
+            x16[n] = work.tile([P, D], BF16, name="x16", bufs=X_LEAD + 3, align_bytes=64)
+            parts = PASSES if n == 0 else 1
+            for part in range(parts):
+                cols = slice(part * D // parts, (part + 1) * D // parts)
+                nc.vector.tensor_tensor(out=x16[n][:, cols], in0=x_raw[g][:, j, cols].bitcast(FP8), in1=scale_all[:, cols], op=ALU.mult)
 
         def turn_x(n):
             words = x16[n][:].bitcast(F32)
-            x_turned[n] = bank("xt")
-            for k in range(PASSES):
+            x_turned[n] = bank("x")
+            pass_words = K_PASS // 2
+            for ps in range(PASSES):
                 for u in range(2):
-                    i = 2 * k + u
-                    nc.tensor.transpose(x_turned[n][:, i * P:(i + 1) * P], words[:, 256 * k + u:256 * (k + 1):2], ident32[:])
+                    slot = 2 * ps + u
+                    nc.tensor.transpose(x_turned[n][:, slot * P:(slot + 1) * P], words[:, pass_words * ps + u:pass_words * (ps + 1):2], ident32[:])
 
         def copy_x(n):
             g, j = divmod(n, TILES)
             if j == 0:
                 x_grouped[g] = work.tile([P, PASSES, GROUP * PACK], BF16, name="x_grouped", align_bytes=64)
-            dst = x_grouped[g][:].bitcast(F32).rearrange("p k (r u) -> p k r u", u=2)[:, :, j * P:(j + 1) * P, :]
-            nc.scalar.copy(out=dst, in_=x_turned[n][:].rearrange("p (k u r) -> p k r u", k=PASSES, u=2))
+            dst = x_grouped[g][:].bitcast(F32).rearrange("p ps (r u) -> p ps r u", u=2)[:, :, j * P:(j + 1) * P, :]
+            nc.scalar.copy(out=dst, in_=x_turned[n][:].rearrange("p (ps u r) -> p ps r u", ps=PASSES, u=2))
 
         def quantize_x(g):
-            x_codes[g] = work.tile([P, PASSES, GROUP], U32, name="x_codes", align_bytes=64)
-            x_scales[g] = work.tile([P, PASSES, GROUP], U8, name="x_scales", align_bytes=64)
-            for k in range(PASSES):
-                nc.vector.quantize_mx(out=x_codes[g][:, k, :].bitcast(FP8X4), scales=x_scales[g][:, k, :],
-                                      in_=x_grouped[g][:, k, :])
+            x_codes[g] = work.tile([P, PASSES, GROUP], U32, name="x_codes", bufs=3, align_bytes=64)
+            x_scales[g] = work.tile([P, PASSES, GROUP], U8, name="x_scales", bufs=3, align_bytes=64)
+            for ps in range(PASSES):
+                nc.vector.quantize_mx(out=x_codes[g][:, ps, :].bitcast(FP8X4), scales=x_scales[g][:, ps, :],
+                                      in_=x_grouped[g][:, ps, :])
 
         def emit(g, c):
-            e_bank[g, c] = bank("et")
+            emission[g, c] = bank("emit")
             cols = slice(c * P, (c + 1) * P)
-            for k in range(PASSES):
-                nc.tensor.matmul_mx(out=e_bank[g, c][:], lhsT=w_codes[k][:, cols].bitcast(FP8X4), lhsT_scale=w_scales[k][:, cols],
-                                    rhs=x_codes[g][:, k, :].bitcast(FP8X4), rhs_scale=x_scales[g][:, k, :],
-                                    start=(k == 0), stop=(k == PASSES - 1))
+            for ps in range(PASSES):
+                nc.tensor.matmul_mx(out=emission[g, c][:], lhsT=w_codes[ps][:, cols].bitcast(FP8X4), lhsT_scale=w_scales[ps][:, cols],
+                                    rhs=x_codes[g][:, ps, :].bitcast(FP8X4), rhs_scale=x_scales[g][:, ps, :],
+                                    start=(ps == 0), stop=(ps == PASSES - 1))
 
         def add_bias(g, c):
-            l = GROUPS[g][0]
+            position = GROUPS[g][0]
             if c == 0:
                 scores_t[g] = work.tile([P, CHUNKS, GROUP], F32, name="scores_t")
-            col = bias_raw[:, c:c + 1] if l == MIDDLE else bias_end[:, (l // 2) * CHUNKS + c:(l // 2) * CHUNKS + c + 1]
-            nc.scalar.activation(out=scores_t[g][:, c, :], in_=e_bank[g, c][:], func=ACT.Identity, bias=col)
+            col = (position // 2) * CHUNKS + c
+            bias = bias_cols[:, c:c + 1] if position == MIDDLE else end_bias[:, col:col + 1]
+            nc.scalar.activation(out=scores_t[g][:, c, :], in_=emission[g, c][:], func=ACT.Identity, bias=bias)
 
-        def turn_scores(n):
+        def turn_scores(n, tag):
             g, j = divmod(n, TILES)
-            rows[n] = bank("rows")
+            turned = bank(tag)
             for c in range(CHUNKS):
-                nc.tensor.transpose(rows[n][:, c * P:(c + 1) * P], scores_t[g][:, c, j * P:(j + 1) * P], ident32[:])
+                nc.tensor.transpose(turned[:, c * P:(c + 1) * P], scores_t[g][:, c, j * P:(j + 1) * P], ident32[:])
+            return turned
 
         def row_max(n):
-            if GROUPS[n // TILES][0] == MIDDLE:
-                neg_scores[n] = keep.tile([P, T], F32, name="neg_scores_%d" % n)
-                nc.vector.tensor_scalar(out=neg_scores[n][:], in0=rows[n][:], scalar1=-1.0, scalar2=None,
-                                        op0=ALU.mult, op1=ALU.min, accum_out=neg_max[:, n:n + 1])
-            else:
-                nc.vector.tensor_reduce(out=neg_max[:, n:n + 1], in_=rows[n][:], axis=AXIS.X, op=ALU.max, negate=True)
+            nc.vector.tensor_reduce(out=neg_max[:, n:n + 1], in_=rows[n][:], axis=AXIS.X, op=ALU.max, negate=True)
 
         def exponentiate(n):
-            if GROUPS[n // TILES][0] == MIDDLE:
+            if is_middle(n):
                 weights[n] = keep.tile([P, T], F32, name="weights_%d" % n)
                 nc.scalar.activation(out=weights[n][:], in_=rows[n][:], func=ACT.Exp, bias=neg_max[:, n:n + 1])
             else:
@@ -223,56 +249,55 @@ def tile_chunkflooredmessagemiddlescore_kernel(tc, x_bytes, x_scale, we, be, end
                                      in_=rows[n][:].rearrange("p (m u s) -> p u m s", u=2, s=2),
                                      func=ACT.Exp, bias=neg_max[:, n:n + 1], accum_out=sums[:, n:n + 1])
 
-        def invert_sum(n):
-            nc.vector.reciprocal(out=inv_sums[:, n:n + 1], in_=sums[:, n:n + 1])
+        def invert_sums(pair):
+            cols = slice(2 * pair, 2 * pair + 2)
+            nc.vector.reciprocal(out=inv_sums[:, cols], in_=sums[:, cols])
 
-        def make_v(n):
-            e = GROUPS[n // TILES][0] // 2
-            v16[n] = work.tile([P, T], BF16, name="v16", bufs=4, align_bytes=64)
-            nc.vector.scalar_tensor_tensor(out=v16[n][:], in0=weights[n][:], scalar=inv_sums[:, n:n + 1],
-                                           in1=gain_all[:, e, :], op0=ALU.mult, op1=ALU.mult)
+        def make_v(pair):
+            for n in (2 * pair, 2 * pair + 1):
+                v16[n] = work.tile([P, T], BF16, name="v16", bufs=4, align_bytes=64)
+                nc.vector.scalar_tensor_tensor(out=v16[n][:], in0=weights[n][:], scalar=inv_sums[:, n:n + 1],
+                                               in1=gain_all[:, GROUPS[n // TILES][0] // 2, :], op0=ALU.mult, op1=ALU.mult)
 
         def turn_v(pair):
-            v_turned[pair] = bank("vt")
-            for i in range(2):
-                words = v16[2 * pair + i][:].bitcast(F32)
+            v_turned[pair] = bank("v")
+            for member in range(2):
+                words = v16[2 * pair + member][:].bitcast(F32)
                 for u in range(2):
-                    s = 2 * i + u
-                    nc.tensor.transpose(v_turned[pair][:, s * P:(s + 1) * P], words[:, u * P:(u + 1) * P], ident32[:])
+                    slot = 2 * member + u
+                    nc.tensor.transpose(v_turned[pair][:, slot * P:(slot + 1) * P], words[:, u * P:(u + 1) * P], ident32[:])
 
         def copy_v(pair):
             v_grouped[pair] = work.tile([P, 2 * P * PACK], BF16, name="v_grouped", align_bytes=64)
-            nc.scalar.copy(out=v_grouped[pair][:].bitcast(F32).rearrange("p (i r u) -> p i r u", i=2, u=2),
-                           in_=v_turned[pair][:].rearrange("p (i u r) -> p i r u", i=2, u=2))
+            nc.scalar.copy(out=v_grouped[pair][:].bitcast(F32).rearrange("p (a r u) -> p a r u", a=2, u=2),
+                           in_=v_turned[pair][:].rearrange("p (a u r) -> p a r u", a=2, u=2))
 
         def quantize_v(pair):
             v_codes[pair] = keep.tile([P, 2 * P], U32, name="v_codes_%d" % pair, align_bytes=64)
             v_scales[pair] = keep.tile([P, 2 * P], U8, name="v_scales_%d" % pair, align_bytes=64)
             nc.vector.quantize_mx(out=v_codes[pair][:].bitcast(FP8X4), scales=v_scales[pair][:], in_=v_grouped[pair][:])
 
-        def tile_of(l, o):
-            h, j = divmod(o, TILES)
-            return GROUPS.index((l, h)) * TILES + j
-
         def pass_messages(o):
+            tag = "emit" if o >= TILES and o % 2 else "x"
             for e in range(2):
-                pair, i = divmod(tile_of(2 * e, o), 2)
-                cols = slice(i * P, (i + 1) * P)
-                m_bank[o, e] = bank(MSG_TAG)
-                nc.tensor.matmul_mx(out=m_bank[o, e][:], lhsT=v_codes[pair][:, cols].bitcast(FP8X4), lhsT_scale=v_scales[pair][:, cols],
+                pair, member = divmod(tile_of(2 * e, o), 2)
+                cols = slice(member * P, (member + 1) * P)
+                message[o, e] = bank(tag)
+                nc.tensor.matmul_mx(out=message[o, e][:], lhsT=v_codes[pair][:, cols].bitcast(FP8X4), lhsT_scale=v_scales[pair][:, cols],
                                     rhs=w_codes[PASSES + e][:].bitcast(FP8X4), rhs_scale=w_scales[PASSES + e][:],
                                     start=True, stop=True)
 
         def floor_messages(o):
             floor0[o] = work.tile([P, T], F32, name="floor0", bufs=3)
             floor1[o] = work.tile([P, T], F32, name="floor1", bufs=3)
-            if o in FLOOR_SET:
-                nc.scalar.activation(out=floor1[o][:], in_=m_bank[o, 1][:], func=ACT.Relu, bias=14.4)
-            nc.scalar.activation(out=floor0[o][:], in_=m_bank[o, 0][:], func=ACT.Relu, scale=1.0 / 16.0, bias=0.9)
-            if o in FLOOR_SET:
+            on_scalar = o % 2 == 0 and o >= SCALAR_FLOORS_FROM
+            if on_scalar:
+                nc.scalar.activation(out=floor1[o][:], in_=message[o, 1][:], func=ACT.Relu, bias=14.4)
+            nc.scalar.activation(out=floor0[o][:], in_=message[o, 0][:], func=ACT.Relu, scale=1.0 / 16.0, bias=0.9)
+            if on_scalar:
                 nc.scalar.activation(out=floor1[o][:], in_=floor1[o][:], func=ACT.Identity, bias=1.6)
             else:
-                nc.vector.tensor_scalar(out=floor1[o][:], in0=m_bank[o, 1][:], scalar1=-14.4, scalar2=16.0, op0=ALU.max, op1=ALU.add)
+                nc.vector.tensor_scalar(out=floor1[o][:], in0=message[o, 1][:], scalar1=-14.4, scalar2=16.0, op0=ALU.max, op1=ALU.add)
 
         def multiply_floors(o):
             product[o] = keep.tile([P, T], F32, name="product_%d" % o)
@@ -284,8 +309,6 @@ def tile_chunkflooredmessagemiddlescore_kernel(tc, x_bytes, x_scale, we, be, end
             nc.vector.scalar_tensor_tensor(out=w[:], in0=w[:], scalar=1.0 / T, in1=product[o][:],
                                            op0=ALU.mult, op1=ALU.mult, accum_out=total[:, o:o + 1])
 
-        out_rows = out.rearrange("(h p j) t -> h j p t", p=P, j=TILES)
-
         def invert_total(o0, o1):
             nc.vector.reciprocal(out=inv_total[:, o0:o1], in_=total[:, o0:o1])
 
@@ -295,94 +318,98 @@ def tile_chunkflooredmessagemiddlescore_kernel(tc, x_bytes, x_scale, we, be, end
         def finish(o):
             n = tile_of(MIDDLE, o)
             nc.vector.scalar_tensor_tensor(out=product[o][:], in0=product[o][:], scalar=neg_max[:, n:n + 1],
-                                           in1=neg_scores[n][:], op0=ALU.add, op1=ALU.subtract)
+                                           in1=middle_rows[o][:], op0=ALU.add, op1=ALU.add)
             nc.sync.dma_start(out=out_rows[o // TILES, o % TILES], in_=product[o][:])
 
-        def log_tick(o):
-            return max(N_TILES + LAG_ROWS + o // LN_PER, sum_tick(o) + 1)
-
         def message_tick(o):
-            ready = max(tile_of(0, o | 1), tile_of(2, o | 1)) + LAG_ROWS + LAG_V + 3
-            return max(MSG_START + MSG_STEP * o, ready + (o & 1))
+            return max(tile_of(0, o | 1), tile_of(2, o | 1)) + PASS_AT + o % 2
 
         def sum_tick(o):
-            return max(message_tick(o) + LAG_G + 1, tile_of(MIDDLE, o) + LAG_ROWS + 1)
+            return max(message_tick(o) + 2, tile_of(MIDDLE, o) + EXP_AT) + 1
 
-        def is_end(n):
-            return 0 <= n < N_TILES and GROUPS[n // TILES][0] != MIDDLE
+        def log_tick(o):
+            return max(N_TILES - 1 + EXP_AT + o // LOGS_PER_TICK, sum_tick(o) + 1)
 
-        interleave_w(0, 0, 1)
-        interleave_w(1, 0, 1)
-        for n in range(LEAD):
+        def due(tick_of, tick):
+            return [o for o in range(N_OUT) if tick_of(o) == tick]
+
+        def x_turn(step):
+            if is_tile(step):
+                turn_x(step)
+
+        def x_scale_ahead(step):
+            if is_tile(step + X_LEAD):
+                scale_x(step + X_LEAD)
+
+        def x_copy(step):
+            if is_tile(step - 1):
+                copy_x(step - 1)
+
+        for i in range(PASSES):
+            interleave_w(i, 0, 1)
+        for n in range(X_LEAD):
             scale_x(n)
-        outs = range(HALVES * TILES)
-        last_tick = max(log_tick(o) for o in outs) + 1
-        for t in range(last_tick + 1):
-            a = t - LAG_ROWS
-            b = a - LAG_V
-            g, c = divmod(t - LAG_QUANT, TILES)
-            emitting = 0 <= g < len(GROUPS)
-            pair_turn = (b - 1) // 2 if (b - 1) % 2 == 1 and is_end(b - 1) else None
-            pair_quant = (b - 2) // 2 if (b - 2) % 2 == 1 and is_end(b - 2) else None
-            messages = [o for o in outs if message_tick(o) == t]
-            if 0 <= a - 1 < N_TILES:
-                exponentiate(a - 1)
-            for o in outs:
-                if log_tick(o) - 1 == t - 1:
-                    take_log(o)
-            if 0 <= a < N_TILES:
-                turn_scores(a)
-            if emitting and c == 0:
-                quantize_x(g)
-            if 0 <= t - 1 < N_TILES:
-                turn_x(t - 1)
-            for rep in range(2 if t in DOUBLE else 0 if t in SKIP else 1):
-                if len(x16) < N_TILES:
-                    scale_x(len(x16))
-            if t in (2, 4):
-                quantize_w(t // 2 - 1)
-            if t == 3:
-                make_bias()
-            if t == GAIN_TICK:
-                make_gain()
-            if pair_turn is not None:
-                turn_v(pair_turn)
-            if 0 <= t - 1 < N_TILES:
-                copy_x(t - 1)
-            if is_end(b):
-                invert_sum(b)
-            if 0 <= a < N_TILES:
-                row_max(a)
-            if is_end(b):
-                make_v(b)
-            if pair_quant is not None:
-                quantize_v(pair_quant)
-            if pair_turn is not None:
-                copy_v(pair_turn)
-            if emitting:
-                emit(g, c)
-            for o in messages:
-                pass_messages(o)
-            if emitting:
-                add_bias(g, c)
-            if 0 <= t - TRANS_START < 8:
-                interleave_w(PASSES + (t - TRANS_START) // 4, (t - TRANS_START) % 4, 4)
-            if t - TRANS_START in (5, 9):
-                quantize_w(PASSES + (t - TRANS_START - 5) // 4)
-            for o in messages:
+        for tick in range(log_tick(N_OUT - 1) + 2):
+            step = tick + len([d for d in DOUBLE_TICKS if d < tick])
+            if is_tile(tick - TURN_SCORES_AT):
+                rows[tick - TURN_SCORES_AT] = turn_scores(tick - TURN_SCORES_AT, "rows")
+            x_turn(step)
+            if closes_pair(tick - TURN_V_AT):
+                turn_v((tick - TURN_V_AT) // 2)
+            if tick == BIAS_SETUP_TICK:
+                turn_bias()
+            if tick == GAIN_SETUP_TICK:
+                spread_gain()
+            if len(x_codes) < len(GROUPS) and step - 1 >= TILES * (len(x_codes) + 1):
+                quantize_x(len(x_codes))
+            if is_tile(tick - EXP_AT):
+                exponentiate(tick - EXP_AT)
+            for o in due(log_tick, tick):
+                take_log(o)
+            if closes_pair(tick - MAKE_V_AT):
+                invert_sums((tick - MAKE_V_AT) // 2)
+            if is_tile(tick - MAX_AT):
+                row_max(tick - MAX_AT)
+            if closes_pair(tick - QUANT_V_AT):
+                quantize_v((tick - QUANT_V_AT) // 2)
+            x_scale_ahead(step)
+            if tick in WE_QUANT_TICKS:
+                quantize_w(WE_QUANT_TICKS.index(tick))
+            if closes_pair(tick - MAKE_V_AT):
+                make_v((tick - MAKE_V_AT) // 2)
+            x_copy(step)
+            if is_tile(tick - BIAS_AT):
+                add_bias(*divmod(tick - BIAS_AT, CHUNKS))
+            if closes_pair(tick - COPY_V_AT):
+                copy_v((tick - COPY_V_AT) // 2)
+            for o in due(message_tick, tick - 1):
                 floor_messages(o)
-            for o in outs:
-                if sum_tick(o) == t:
-                    sum_tags(o)
-            for o in outs:
-                if message_tick(o) + LAG_G == t:
-                    multiply_floors(o)
-
-            for o in outs:
-                if sum_tick(o) == t and o >= TILES:
-                    invert_total(o, o + 1)
-            if sum_tick(TILES - 1) + 1 == t:
-                invert_total(0, TILES)
-            for o in outs:
-                if log_tick(o) == t:
-                    finish(o)
+            if tick == BIAS_SETUP_TICK + 1:
+                copy_bias()
+            if tick == GAIN_SETUP_TICK + 1:
+                copy_gain()
+            if 0 <= tick - TRANS_TICK < 2 * TRANS_PARTS:
+                e, part = divmod(tick - TRANS_TICK, TRANS_PARTS)
+                interleave_w(PASSES + e, part, TRANS_PARTS)
+            for e in range(2):
+                if tick == TRANS_TICK + (e + 1) * TRANS_PARTS + 1:
+                    quantize_w(PASSES + e)
+            for o in due(sum_tick, tick):
+                sum_tags(o)
+            for o in due(message_tick, tick - 2):
+                multiply_floors(o)
+            for o in due(sum_tick, tick):
+                if o >= TILES - 1:
+                    invert_total(0 if o == TILES - 1 else o, o + 1)
+            for o in due(log_tick, tick - 1):
+                finish(o)
+            for o in due(log_tick, tick):
+                middle_rows[o] = turn_scores(tile_of(MIDDLE, o), "v" if o % 4 == 3 else "rows")
+            if tick in DOUBLE_TICKS:
+                x_turn(step + 1)
+                x_scale_ahead(step + 1)
+                x_copy(step + 1)
+            if is_tile(tick - EMIT_AT):
+                emit(*divmod(tick - EMIT_AT, CHUNKS))
+            for o in due(message_tick, tick):
+                pass_messages(o)

@@ -57,7 +57,7 @@ def tile_chunkflooredmessagemiddlescore_kernel(tc, x_bytes, x_scale, we, be, end
         keep = ctx.enter_context(tc.tile_pool(name="keep", bufs=1))
         work = ctx.enter_context(tc.tile_pool(name="work", bufs=2))
         psum = ctx.enter_context(tc.psum_pool(name="psum", bufs=1))
-        ctx.enter_context(tc.manual_schedule())
+        ctx.enter_context(tc.manual_schedule(engines={mybir.EngineType.Activation, mybir.EngineType.PE, mybir.EngineType.SP}))
 
         def bank(tag, shape=(P, T), dtype=F32):
             return psum.tile(list(shape), dtype, name=tag, tag=tag, bufs=BANKS[tag])
@@ -209,9 +209,9 @@ def tile_chunkflooredmessagemiddlescore_kernel(tc, x_bytes, x_scale, we, be, end
         def quantize_x(g):
             x_codes[g] = work.tile([P, PASSES, GROUP], U32, name="x_codes", bufs=3, align_bytes=64)
             x_scales[g] = work.tile([P, PASSES, GROUP], U8, name="x_scales", bufs=3, align_bytes=64)
-            for ps in range(PASSES):
-                nc.vector.quantize_mx(out=x_codes[g][:, ps, :].bitcast(FP8X4), scales=x_scales[g][:, ps, :],
-                                      in_=x_grouped[g][:, ps, :])
+            nc.vector.quantize_mx(out=x_codes[g][:].rearrange("p ps r -> p (ps r)").bitcast(FP8X4),
+                                  scales=x_scales[g][:].rearrange("p ps r -> p (ps r)"),
+                                  in_=x_grouped[g][:].rearrange("p ps r -> p (ps r)"))
 
         def emit(g, c):
             emission[g, c] = bank("emit")

from contextlib import ExitStack

import concourse.mybir as mybir
from concourse.masks import make_identity

L, B, D, T = 3, 1024, 1024, 512
FLOPS = 2 * L * B * D * T + 2 * 2 * B * T * T

F32 = mybir.dt.float32
BF16 = mybir.dt.bfloat16
U32 = mybir.dt.uint32
U8 = mybir.dt.uint8
FP8 = mybir.dt.float8_e4m3fn
FP8X4 = mybir.dt.float8_e4m3fn_x4
ACT = mybir.ActivationFunctionType
ALU = mybir.AluOpType
AXIS = mybir.AxisListType

P = 128
PACK = 4
K_PASS = P * PACK
PASSES = D // K_PASS
GROUP = 512
TILES = GROUP // P
CHUNKS = T // P
MIDDLE = 1
GROUPS = [(0, 0), (2, 0), (0, 1), (2, 1), (MIDDLE, 0), (MIDDLE, 1)]
N_TILES = len(GROUPS) * TILES
N_OUT = B // P

EMIT_AT = TILES + 1
BIAS_AT = EMIT_AT + 1
TURN_SCORES_AT = BIAS_AT + CHUNKS
MAX_AT = TURN_SCORES_AT + 1
EXP_AT = MAX_AT + 1
MAKE_V_AT = EXP_AT + 1
TURN_V_AT = MAKE_V_AT + 1
COPY_V_AT = TURN_V_AT + 1
QUANT_V_AT = COPY_V_AT + 1
PASS_AT = QUANT_V_AT + 1
DOUBLE_TICKS = range(BIAS_AT, TURN_SCORES_AT)
X_LEAD = 2
WE_QUANT_TICKS = (2, 4)
BIAS_SETUP_TICK = BIAS_AT - 3
GAIN_SETUP_TICK = MAKE_V_AT - 2
TRANS_TICK = 4
TRANS_PARTS = 4
SCALAR_FLOORS_FROM = 2
LOGS_PER_TICK = 2

BANKS = {"x": 2, "emit": 2, "rows": 3, "v": 1}


def tile_chunkflooredmessagemiddlescore_kernel(tc, x_bytes, x_scale, we, be, ends, gain, trans, out):
    nc = tc.nc
    with ExitStack() as ctx:
        keep = ctx.enter_context(tc.tile_pool(name="keep", bufs=1))
        work = ctx.enter_context(tc.tile_pool(name="work", bufs=2))
        psum = ctx.enter_context(tc.psum_pool(name="psum", bufs=1))
        ctx.enter_context(tc.manual_schedule(engines={mybir.EngineType.Activation, mybir.EngineType.PE, mybir.EngineType.SP}))

        def bank(tag, shape=(P, T), dtype=F32):
            return psum.tile(list(shape), dtype, name=tag, tag=tag, bufs=BANKS[tag])

        n_weights = PASSES + 2
        x_raw = [keep.tile([P, TILES, D], U8, name="x_bytes_%d" % g, align_bytes=64) for g in range(len(GROUPS))]
        w_raw = [keep.tile([P, PACK, T], BF16, name="w_raw_%d" % i, align_bytes=64) for i in range(n_weights)]
        scale_cols = keep.tile([P, PASSES * PACK], F32, name="scale_cols")
        bias_rows = keep.tile([P, P], BF16, name="bias_rows")
        gain_cols = keep.tile([P, 2, PACK], BF16, name="gain_cols")
        ident32 = keep.tile([P, P], F32, name="ident32")
        ident16 = keep.tile([P, P], BF16, name="ident16")

        def load_x(g, j0, j1):
            position, half = GROUPS[g]
            tokens = x_bytes[position, half * GROUP:(half + 1) * GROUP, :].rearrange("(p j) k -> p j k", j=TILES)
            nc.sync.dma_start(out=x_raw[g][:, j0:j1, :], in_=tokens[:, j0:j1, :])

        def load_w(i):
            matrix = we[i * K_PASS:(i + 1) * K_PASS, :] if i < PASSES else trans[i - PASSES]
            nc.sync.dma_start(out=w_raw[i][:], in_=matrix.rearrange("(p t) n -> p t n", t=PACK))

        make_identity(nc, ident32[:])
        make_identity(nc, ident16[:])
        nc.vector.memset(bias_rows[:], 0.0)
        nc.sync.dma_start(out=scale_cols[:].rearrange("p (ps t) -> p ps t", ps=PASSES),
                          in_=x_scale.rearrange("a b (ps p t) -> p (a b ps) t", ps=PASSES, t=PACK))
        load_x(0, 0, 1)
        load_w(0)
        load_x(0, 1, 2)
        load_w(1)
        load_x(0, 2, TILES)
        load_x(1, 0, TILES)
        nc.sync.dma_start(out=bias_rows[0:CHUNKS, :], in_=be.rearrange("(c q) -> c q", q=P))
        nc.sync.dma_start(out=bias_rows[CHUNKS:3 * CHUNKS, :], in_=ends.rearrange("e (c q) -> (e c) q", q=P))
        nc.sync.dma_start(out=gain_cols[:], in_=gain.rearrange("e (p t) -> p e t", t=PACK))
        load_w(PASSES)
        load_x(2, 0, TILES)
        load_w(PASSES + 1)
        for g in range(3, len(GROUPS)):
            load_x(g, 0, TILES)

        scale_all = keep.tile([P, D], F32, name="scale_all")
        for ps in range(PASSES):
            spread = bank("rows")
            for t in range(PACK):
                col = PACK * ps + t
                nc.tensor.transpose(spread[:, t * P:(t + 1) * P], scale_cols[:, col:col + 1].to_broadcast([P, P]), ident32[:])
            dst = scale_all[:, ps * K_PASS:(ps + 1) * K_PASS].rearrange("p (q t) -> p q t", t=PACK)
            src = spread[:].rearrange("p (t q) -> p q t", t=PACK)
            if ps == 0:
                nc.vector.tensor_copy(out=dst, in_=src)
            else:
                nc.scalar.copy(out=dst, in_=src)

        w_codes = [keep.tile([P, T], U32, name="w_codes_%d" % i, align_bytes=64) for i in range(n_weights)]
        w_scales = [keep.tile([P, T], U8, name="w_scales_%d" % i, align_bytes=64) for i in range(n_weights)]
        w_grouped = {}

        def interleave_w(i, part, parts):
            if part == 0:
                w_grouped[i] = work.tile([P, T, PACK], BF16, name="w_grouped", align_bytes=64)
            cols = slice(part * T // parts, (part + 1) * T // parts)
            nc.scalar.copy(out=w_grouped[i][:, cols, :].rearrange("p (c r) t -> p c t r", r=4),
                           in_=w_raw[i][:, :, cols].rearrange("p t (c r) -> p c t r", r=4))

        def quantize_w(i):
            nc.vector.quantize_mx(out=w_codes[i][:].bitcast(FP8X4), scales=w_scales[i][:],
                                  in_=w_grouped[i][:].rearrange("p n t -> p (n t)"))

        bias_cols = keep.tile([P, 3 * CHUNKS], F32, name="bias_cols")
        end_bias = keep.tile([P, 2 * CHUNKS], F32, name="end_bias")

        bias_bank = []

        def turn_bias():
            bias_bank.append(bank("v", (P, P), BF16))
            nc.tensor.transpose(bias_bank[0][:], bias_rows[:], ident16[:])

        def copy_bias():
            nc.scalar.copy(out=bias_cols[:], in_=bias_bank[0][:, 0:3 * CHUNKS])
            for e in range(2):
                nc.gpsimd.tensor_tensor(out=end_bias[:, e * CHUNKS:(e + 1) * CHUNKS], in0=bias_cols[:, 0:CHUNKS],
                                        in1=bias_cols[:, (e + 1) * CHUNKS:(e + 2) * CHUNKS], op=ALU.add)

        gain_all = keep.tile([P, 2, T], F32, name="gain_all")
        gain_bank = []

        def spread_gain():
            gain_bank.append(bank("v", (P, 2, PACK, P), BF16))
            for e in range(2):
                for t in range(PACK):
                    nc.tensor.transpose(gain_bank[0][:, e, t, :], gain_cols[:, e, t:t + 1].to_broadcast([P, P]), ident16[:])

        def copy_gain():
            for e in range(2):
                nc.scalar.activation(out=gain_all[:, e, :].rearrange("p (u m s) -> p u m s", u=2, s=2),
                                     in_=gain_bank[0][:, e].rearrange("p (u s) m -> p u m s", u=2),
                                     func=ACT.Copy, scale=float(T))

        neg_max = keep.tile([P, N_TILES], F32, name="neg_max")
        sums = keep.tile([P, N_TILES], F32, name="sums")
        inv_sums = keep.tile([P, N_TILES], F32, name="inv_sums")
        total = keep.tile([P, N_OUT], F32, name="total")
        inv_total = keep.tile([P, N_OUT], F32, name="inv_total")
        x16, x_turned, x_grouped, x_codes, x_scales = {}, {}, {}, {}, {}
        emission, scores_t, rows, weights = {}, {}, {}, {}
        v16, v_turned, v_grouped, v_codes, v_scales = {}, {}, {}, {}, {}
        message, floor0, floor1, product, middle_rows = {}, {}, {}, {}, {}
        out_rows = out.rearrange("(h p j) t -> h j p t", p=P, j=TILES)

        def is_tile(n):
            return 0 <= n < N_TILES

        def is_middle(n):
            return GROUPS[n // TILES][0] == MIDDLE

        def closes_pair(n):
            return is_tile(n) and not is_middle(n) and n % 2 == 1

        def tile_of(position, o):
            half, j = divmod(o, TILES)
            return GROUPS.index((position, half)) * TILES + j

        def scale_x(n):
            g, j = divmod(n, TILES)
            x16[n] = work.tile([P, D], BF16, name="x16", bufs=X_LEAD + 3, align_bytes=64)
            parts = PASSES if n == 0 else 1
            for part in range(parts):
                cols = slice(part * D // parts, (part + 1) * D // parts)
                nc.vector.tensor_tensor(out=x16[n][:, cols], in0=x_raw[g][:, j, cols].bitcast(FP8), in1=scale_all[:, cols], op=ALU.mult)

        def turn_x(n):
            words = x16[n][:].bitcast(F32)
            x_turned[n] = bank("x")
            pass_words = K_PASS // 2
            for ps in range(PASSES):
                for u in range(2):
                    slot = 2 * ps + u
                    nc.tensor.transpose(x_turned[n][:, slot * P:(slot + 1) * P], words[:, pass_words * ps + u:pass_words * (ps + 1):2], ident32[:])

        def copy_x(n):
            g, j = divmod(n, TILES)
            if j == 0:
                x_grouped[g] = work.tile([P, PASSES, GROUP * PACK], BF16, name="x_grouped", align_bytes=64)
            dst = x_grouped[g][:].bitcast(F32).rearrange("p ps (r u) -> p ps r u", u=2)[:, :, j * P:(j + 1) * P, :]
            nc.scalar.copy(out=dst, in_=x_turned[n][:].rearrange("p (ps u r) -> p ps r u", ps=PASSES, u=2))

        def quantize_x(g):
            x_codes[g] = work.tile([P, PASSES, GROUP], U32, name="x_codes", bufs=3, align_bytes=64)
            x_scales[g] = work.tile([P, PASSES, GROUP], U8, name="x_scales", bufs=3, align_bytes=64)
            nc.vector.quantize_mx(out=x_codes[g][:].rearrange("p ps r -> p (ps r)").bitcast(FP8X4),
                                  scales=x_scales[g][:].rearrange("p ps r -> p (ps r)"),
                                  in_=x_grouped[g][:].rearrange("p ps r -> p (ps r)"))

        def emit(g, c):
            emission[g, c] = bank("emit")
            cols = slice(c * P, (c + 1) * P)
            for ps in range(PASSES):
                nc.tensor.matmul_mx(out=emission[g, c][:], lhsT=w_codes[ps][:, cols].bitcast(FP8X4), lhsT_scale=w_scales[ps][:, cols],
                                    rhs=x_codes[g][:, ps, :].bitcast(FP8X4), rhs_scale=x_scales[g][:, ps, :],
                                    start=(ps == 0), stop=(ps == PASSES - 1))

        def add_bias(g, c):
            position = GROUPS[g][0]
            if c == 0:
                scores_t[g] = work.tile([P, CHUNKS, GROUP], F32, name="scores_t")
            col = (position // 2) * CHUNKS + c
            bias = bias_cols[:, c:c + 1] if position == MIDDLE else end_bias[:, col:col + 1]
            nc.scalar.activation(out=scores_t[g][:, c, :], in_=emission[g, c][:], func=ACT.Identity, bias=bias)

        def turn_scores(n, tag):
            g, j = divmod(n, TILES)
            turned = bank(tag)
            for c in range(CHUNKS):
                nc.tensor.transpose(turned[:, c * P:(c + 1) * P], scores_t[g][:, c, j * P:(j + 1) * P], ident32[:])
            return turned

        def row_max(n):
            nc.vector.tensor_reduce(out=neg_max[:, n:n + 1], in_=rows[n][:], axis=AXIS.X, op=ALU.max, negate=True)

        def exponentiate(n):
            if is_middle(n):
                weights[n] = keep.tile([P, T], F32, name="weights_%d" % n)
                nc.scalar.activation(out=weights[n][:], in_=rows[n][:], func=ACT.Exp, bias=neg_max[:, n:n + 1])
            else:
                weights[n] = work.tile([P, T], F32, name="weights", bufs=4)
                nc.scalar.activation(out=weights[n][:].rearrange("p (u m s) -> p u m s", u=2, s=2),
                                     in_=rows[n][:].rearrange("p (m u s) -> p u m s", u=2, s=2),
                                     func=ACT.Exp, bias=neg_max[:, n:n + 1], accum_out=sums[:, n:n + 1])

        def invert_sums(pair):
            cols = slice(2 * pair, 2 * pair + 2)
            nc.vector.reciprocal(out=inv_sums[:, cols], in_=sums[:, cols])

        def make_v(pair):
            for n in (2 * pair, 2 * pair + 1):
                v16[n] = work.tile([P, T], BF16, name="v16", bufs=4, align_bytes=64)
                nc.vector.scalar_tensor_tensor(out=v16[n][:], in0=weights[n][:], scalar=inv_sums[:, n:n + 1],
                                               in1=gain_all[:, GROUPS[n // TILES][0] // 2, :], op0=ALU.mult, op1=ALU.mult)

        def turn_v(pair):
            v_turned[pair] = bank("v")
            for member in range(2):
                words = v16[2 * pair + member][:].bitcast(F32)
                for u in range(2):
                    slot = 2 * member + u
                    nc.tensor.transpose(v_turned[pair][:, slot * P:(slot + 1) * P], words[:, u * P:(u + 1) * P], ident32[:])

        def copy_v(pair):
            v_grouped[pair] = work.tile([P, 2 * P * PACK], BF16, name="v_grouped", align_bytes=64)
            nc.scalar.copy(out=v_grouped[pair][:].bitcast(F32).rearrange("p (a r u) -> p a r u", a=2, u=2),
                           in_=v_turned[pair][:].rearrange("p (a u r) -> p a r u", a=2, u=2))

        def quantize_v(pair):
            v_codes[pair] = keep.tile([P, 2 * P], U32, name="v_codes_%d" % pair, align_bytes=64)
            v_scales[pair] = keep.tile([P, 2 * P], U8, name="v_scales_%d" % pair, align_bytes=64)
            nc.vector.quantize_mx(out=v_codes[pair][:].bitcast(FP8X4), scales=v_scales[pair][:], in_=v_grouped[pair][:])

        def pass_messages(o):
            tag = "emit" if o >= TILES and o % 2 else "x"
            for e in range(2):
                pair, member = divmod(tile_of(2 * e, o), 2)
                cols = slice(member * P, (member + 1) * P)
                message[o, e] = bank(tag)
                nc.tensor.matmul_mx(out=message[o, e][:], lhsT=v_codes[pair][:, cols].bitcast(FP8X4), lhsT_scale=v_scales[pair][:, cols],
                                    rhs=w_codes[PASSES + e][:].bitcast(FP8X4), rhs_scale=w_scales[PASSES + e][:],
                                    start=True, stop=True)

        def floor_messages(o):
            floor0[o] = work.tile([P, T], F32, name="floor0", bufs=3)
            floor1[o] = work.tile([P, T], F32, name="floor1", bufs=3)
            on_scalar = o % 2 == 0 and o >= SCALAR_FLOORS_FROM
            if on_scalar:
                nc.scalar.activation(out=floor1[o][:], in_=message[o, 1][:], func=ACT.Relu, bias=14.4)
            nc.scalar.activation(out=floor0[o][:], in_=message[o, 0][:], func=ACT.Relu, scale=1.0 / 16.0, bias=0.9)
            if on_scalar:
                nc.scalar.activation(out=floor1[o][:], in_=floor1[o][:], func=ACT.Identity, bias=1.6)
            else:
                nc.vector.tensor_scalar(out=floor1[o][:], in0=message[o, 1][:], scalar1=-14.4, scalar2=16.0, op0=ALU.max, op1=ALU.add)

        def multiply_floors(o):
            product[o] = keep.tile([P, T], F32, name="product_%d" % o)
            nc.vector.scalar_tensor_tensor(out=product[o][:], in0=floor0[o][:], scalar=0.1, in1=floor1[o][:],
                                           op0=ALU.add, op1=ALU.mult)

        def sum_tags(o):
            w = weights[tile_of(MIDDLE, o)]
            nc.vector.scalar_tensor_tensor(out=w[:], in0=w[:], scalar=1.0 / T, in1=product[o][:],
                                           op0=ALU.mult, op1=ALU.mult, accum_out=total[:, o:o + 1])

        def invert_total(o0, o1):
            nc.vector.reciprocal(out=inv_total[:, o0:o1], in_=total[:, o0:o1])

        def take_log(o):
            nc.scalar.activation(out=product[o][:], in_=product[o][:], func=ACT.Ln, scale=inv_total[:, o:o + 1])

        def finish(o):
            n = tile_of(MIDDLE, o)
            nc.vector.scalar_tensor_tensor(out=product[o][:], in0=product[o][:], scalar=neg_max[:, n:n + 1],
                                           in1=middle_rows[o][:], op0=ALU.add, op1=ALU.add)
            nc.sync.dma_start(out=out_rows[o // TILES, o % TILES], in_=product[o][:])

        def message_tick(o):
            return max(tile_of(0, o | 1), tile_of(2, o | 1)) + PASS_AT + o % 2

        def sum_tick(o):
            return max(message_tick(o) + 2, tile_of(MIDDLE, o) + EXP_AT) + 1

        def log_tick(o):
            return max(N_TILES - 1 + EXP_AT + o // LOGS_PER_TICK, sum_tick(o) + 1)

        def due(tick_of, tick):
            return [o for o in range(N_OUT) if tick_of(o) == tick]

        def x_turn(step):
            if is_tile(step):
                turn_x(step)

        def x_scale_ahead(step):
            if is_tile(step + X_LEAD):
                scale_x(step + X_LEAD)

        def x_copy(step):
            if is_tile(step - 1):
                copy_x(step - 1)

        for i in range(PASSES):
            interleave_w(i, 0, 1)
        for n in range(X_LEAD):
            scale_x(n)
        for tick in range(log_tick(N_OUT - 1) + 2):
            step = tick + len([d for d in DOUBLE_TICKS if d < tick])
            if is_tile(tick - TURN_SCORES_AT):
                rows[tick - TURN_SCORES_AT] = turn_scores(tick - TURN_SCORES_AT, "rows")
            x_turn(step)
            if closes_pair(tick - TURN_V_AT):
                turn_v((tick - TURN_V_AT) // 2)
            if tick == BIAS_SETUP_TICK:
                turn_bias()
            if tick == GAIN_SETUP_TICK:
                spread_gain()
            if len(x_codes) < len(GROUPS) and step - 1 >= TILES * (len(x_codes) + 1):
                quantize_x(len(x_codes))
            if is_tile(tick - EXP_AT):
                exponentiate(tick - EXP_AT)
            for o in due(log_tick, tick):
                take_log(o)
            if closes_pair(tick - MAKE_V_AT):
                invert_sums((tick - MAKE_V_AT) // 2)
            if is_tile(tick - MAX_AT):
                row_max(tick - MAX_AT)
            if closes_pair(tick - QUANT_V_AT):
                quantize_v((tick - QUANT_V_AT) // 2)
            x_scale_ahead(step)
            if tick in WE_QUANT_TICKS:
                quantize_w(WE_QUANT_TICKS.index(tick))
            if closes_pair(tick - MAKE_V_AT):
                make_v((tick - MAKE_V_AT) // 2)
            x_copy(step)
            if is_tile(tick - BIAS_AT):
                add_bias(*divmod(tick - BIAS_AT, CHUNKS))
            if closes_pair(tick - COPY_V_AT):
                copy_v((tick - COPY_V_AT) // 2)
            for o in due(message_tick, tick - 1):
                floor_messages(o)
            if tick == BIAS_SETUP_TICK + 1:
                copy_bias()
            if tick == GAIN_SETUP_TICK + 1:
                copy_gain()
            if 0 <= tick - TRANS_TICK < 2 * TRANS_PARTS:
                e, part = divmod(tick - TRANS_TICK, TRANS_PARTS)
                interleave_w(PASSES + e, part, TRANS_PARTS)
            for e in range(2):
                if tick == TRANS_TICK + (e + 1) * TRANS_PARTS + 1:
                    quantize_w(PASSES + e)
            for o in due(sum_tick, tick):
                sum_tags(o)
            for o in due(message_tick, tick - 2):
                multiply_floors(o)
            for o in due(sum_tick, tick):
                if o >= TILES - 1:
                    invert_total(0 if o == TILES - 1 else o, o + 1)
            for o in due(log_tick, tick - 1):
                finish(o)
            for o in due(log_tick, tick):
                middle_rows[o] = turn_scores(tile_of(MIDDLE, o), "v" if o % 4 == 3 else "rows")
            if tick in DOUBLE_TICKS:
                x_turn(step + 1)
                x_scale_ahead(step + 1)
                x_copy(step + 1)
            if is_tile(tick - EMIT_AT):
                emit(*divmod(tick - EMIT_AT, CHUNKS))
            for o in due(message_tick, tick):
                pass_messages(o)
